import numpy as np
import ml_dtypes


def mxq(x, axis, fmt="e4m3"):
    dtype, down = {"e4m3": (ml_dtypes.float8_e4m3fn, 7), "e5m2": (ml_dtypes.float8_e5m2, 14)}[fmt]
    v = np.moveaxis(np.asarray(x, np.float32).astype(ml_dtypes.bfloat16).astype(np.float64), axis, -1)
    blocks = v.reshape(v.shape[:-1] + (-1, 32))
    amax = np.abs(blocks).max(-1, keepdims=True)
    byte = np.maximum(np.where(amax > 0, np.frexp(amax)[1] - 1 + 127, 0) - down, 1)
    scale = np.exp2(byte - 127.0)
    codes = (blocks / scale).astype(np.float32).astype(dtype).astype(np.float64)
    return np.moveaxis((codes * scale).reshape(v.shape), -1, axis)


WIDE = False


def mx_kscale(k):
    if not WIDE:
        return np.ones(k)
    levels = np.array([10, -10, 5, -5, 0])
    if k % 512:
        return np.exp2(np.random.permutation(np.resize(levels, k // 32))).repeat(32)
    a = np.empty((k // 512, 16))
    for p in range(k // 512):
        a[p, :8] = np.random.permutation(np.resize(levels, 8))
        for g in range(8):
            far = levels[np.abs(levels - a[p, g]) >= 10]
            a[p, g + 8] = far[np.random.randint(len(far))]
    return np.exp2(a.ravel()).repeat(32)


def f64(x):
    return np.asarray(x).astype(np.float64)


def striped(idx):
    return np.tile(np.asarray(idx).reshape(-1, 16).T, (8, 1)).astype(np.uint16)


def unstriped(offs):
    return offs[:16].T.reshape(-1).astype(np.int64)


E2M1 = np.array([0.0, 0.5, 1.0, 1.5, 2.0, 3.0, 4.0, 6.0, -0.0, -0.5, -1.0, -1.5, -2.0, -3.0, -4.0, -6.0])


def pack_weight(w, fmt):
    k, n = w.shape
    w = f64(np.asarray(w, np.float32).astype(ml_dtypes.bfloat16)).reshape(k // 32, 32, n)
    amax = np.abs(w).max(1)
    if fmt == "e4m3":
        byte = np.frexp(amax)[1] - 1 + 127 - 7
    else:
        mant, ex = np.frexp(amax / 6.0)
        byte = np.where(mant > 0.5, ex, ex - 1) + 127
    byte = np.clip(np.where(amax > 0, byte, 1), 1, 254)
    scaled = (w * np.exp2(127.0 - byte)[:, None, :]).reshape(k, n).astype(np.float32)
    by_word = np.ascontiguousarray(scaled.reshape(k // 512, 128, 4, n).transpose(0, 1, 3, 2))
    if fmt == "e4m3":
        words = by_word.astype(ml_dtypes.float8_e4m3fn).view(np.uint8)
    else:
        c = by_word.astype(ml_dtypes.float4_e2m1fn).view(np.uint8) & 0xF
        words = (c[..., 0::2] | (c[..., 1::2] << 4)).reshape(k // 512, 128, 2 * n)
    return np.ascontiguousarray(words), np.ascontiguousarray(byte.astype(np.uint8).reshape(k // 512, 16, n))


def unpack_weight(words, scales, fmt):
    g, _, n = scales.shape
    words = np.ascontiguousarray(words).reshape(g, 128, n, -1)
    if fmt == "e4m3":
        vals = words.view(ml_dtypes.float8_e4m3fn).astype(np.float64)
    else:
        nib = np.empty((g, 128, n, 4), np.uint8)
        nib[..., 0::2] = words & 0xF
        nib[..., 1::2] = words >> 4
        vals = E2M1[nib]
    vals = vals * np.repeat(np.exp2(scales.astype(np.float64) - 127.0), 8, axis=1)[..., None]
    return vals.transpose(0, 1, 3, 2).reshape(g * 512, n)


def bf(x):
    return np.asarray(x, np.float32).astype(ml_dtypes.bfloat16)


def planes(Y):
    r, m = Y.shape
    b = f64(bf(Y)).reshape(r // 32, 32, m)
    amax = np.abs(b).max(1)
    byte = np.clip(np.where(amax > 0, np.frexp(amax)[1] - 1 + 127 - 7, 1), 1, 254)
    codes = (b * np.exp2(127.0 - byte)[:, None, :]).reshape(r, m).astype(np.float32).astype(ml_dtypes.float8_e4m3fn).view(np.uint8)
    words = codes.reshape(r // 512, 128, 4, m).transpose(0, 1, 3, 2)
    return np.ascontiguousarray(words), np.ascontiguousarray(byte.astype(np.uint8).reshape(r // 512, 16, m))


K, B, T, I, Q = 512, 512, 2048, 512, 128


def setup_inputs():
    n = np.random.standard_normal
    idx = np.random.permutation(T)[:I]
    fk = mx_kscale(K)
    fi = mx_kscale(I)
    embp = pack_weight(n((K, T)) / fk[:, None], "e2m1")
    return {
        "qemb": (n((K, Q)) * fk[:, None]).astype(np.float32),
        "wq": (n((K, B)) * 1 / np.sqrt(K) / fk[:, None]).astype(np.float32),
        "emb_words": embp[0],
        "emb_scales": embp[1],
        "wi": (n((K, B)) * 1 / np.sqrt(K) * fk[:, None]).astype(np.float32),
        "isc": (np.random.uniform(0.5, 2.0, (I, 1)) * fi[:, None]).astype(np.float32),
        "dsc": (n((I, Q)) * 0.06 / fi[:, None]).astype(np.float32),
        "gain": (np.random.uniform(0.5, 2.0, (B, 1))).astype(np.float32),
        "old": (n((B, Q)) * 0.5).astype(np.float32),
        "offs": striped(idx),
    }


def reference(qemb, wq, emb_words, emb_scales, wi, isc, dsc, gain, old, offs):
    idx = unstriped(offs)
    embu = unpack_weight(emb_words, emb_scales, "e2m1")
    wqq = mxq(f64(wq), 0, "e4m3")
    qembq = mxq(f64(qemb), 0, "e4m3")
    z = wqq.T @ qembq
    wiq = mxq(f64(wi), 0, "e4m3")
    embidxg = embu[:, idx]
    g1 = wiq.T @ embidxg
    h1 = np.tanh(g1)
    ht = h1.T
    hs = ht * f64(isc)
    hsq = mxq(hs, 0, "e4m3")
    dscq = mxq(f64(dsc), 0, "e4m3")
    gh = hsq.T @ dscq
    y = gh * (1.0 - np.square(np.tanh(z))) * f64(gain) + f64(old)
    words, scales = planes(y)
    return y, words, scales

@@ -1,0 +1,202 @@
+from contextlib import ExitStack
+
+import concourse.mybir as mybir
+
+K, B, T, I, Q = 512, 512, 2048, 512, 128
+FLOPS = 2 * K * B * Q + 2 * K * B * I + 2 * I * B * Q
+
+F32 = mybir.dt.float32
+BF16 = mybir.dt.bfloat16
+I32 = mybir.dt.int32
+U32 = mybir.dt.uint32
+U16 = mybir.dt.uint16
+U8 = mybir.dt.uint8
+FP8X4 = mybir.dt.float8_e4m3fn_x4
+FP4X4 = mybir.dt.float4_e2m1fn_x4
+ACT = mybir.ActivationFunctionType
+ALU = mybir.AluOpType
+
+P = 128
+PACK = 4
+HALF = B // 2
+
+
+def tile_attend_bsoftcodes_pl_kernel(
+    tc, qemb, wq, emb_words, emb_scales, wi, isc, dsc, gain, old, offs, out_0, out_1, out_2
+):
+    nc = tc.nc
+    with ExitStack() as ctx:
+        sb = ctx.enter_context(tc.tile_pool(name="sb", bufs=1))
+        ps = ctx.enter_context(tc.psum_pool(name="ps", bufs=1))
+
+        def tile(name, shape, dtype):
+            return sb.tile(shape, dtype, name=name, align_bytes=64)
+
+        def rows4(src):
+            return src.rearrange("(p j) w -> p j w", j=PACK)
+
+        offsets = tile("offsets", [P, I // 16], U16)
+        store_scales = tile("store_scales", [P, T], U8)
+        store_words = tile("store_words", [P, T], U16)
+        wi_raw = [tile("wi_raw%d" % h, [P, PACK, HALF], F32) for h in range(2)]
+        warm_in = sb.tile([P, 1], F32, name="warm_in", tag="late", align_bytes=64)
+        warm_out = tile("warm_out", [P, 1], F32)
+
+        nc.vector.memset(store_scales[:].bitcast(I32), 0)
+        nc.vector.memset(warm_in[:], 0.0)
+        nc.sync.dma_start(offsets[:], offs)
+        for g in range(4):
+            nc.scalar.dma_start(
+                store_scales[32 * g : 32 * g + 4, :].bitcast(I32),
+                emb_scales[0, 4 * g : 4 * g + 4, :].bitcast(I32),
+            )
+        nc.sync.dma_start(store_words[:].bitcast(I32), emb_words[0].bitcast(I32))
+        for h in range(2):
+            nc.sync.dma_start(wi_raw[h][:], rows4(wi[:, h * HALF : (h + 1) * HALF]))
+        nc.scalar.activation(warm_out[:], warm_in[:], ACT.Tanh)
+
+        late = sb.tile([P, 2 * PACK * HALF + 3 * PACK * Q + 16], F32, name="late", tag="late", align_bytes=64)
+
+        def part_of_late(start, width):
+            return late[:, start : start + PACK * width].rearrange("p (j w) -> p j w", j=PACK)
+
+        wq_raw = [part_of_late(h * PACK * HALF, HALF) for h in range(2)]
+        qemb_raw, dsc_raw, old_sb = [part_of_late(PACK * B + n * PACK * Q, Q) for n in range(3)]
+        vectors = PACK * B + 3 * PACK * Q
+        isc_sb = late[:, vectors : vectors + PACK]
+        gain_sb = late[:, vectors + 8 : vectors + 8 + PACK]
+        nc.sync.dma_start(isc_sb, isc.rearrange("(p j) o -> p (j o)", j=PACK))
+        nc.sync.dma_start(qemb_raw, rows4(qemb))
+        for h in range(2):
+            nc.sync.dma_start(wq_raw[h], rows4(wq[:, h * HALF : (h + 1) * HALF]))
+        nc.sync.dma_start(dsc_raw, rows4(dsc))
+        nc.sync.dma_start(gain_sb, gain.rearrange("(p j) o -> p (j o)", j=PACK))
+        nc.sync.dma_start(old_sb, rows4(old))
+
+        def weave(copy, dst, src):
+            copy(
+                dst.rearrange("p (c i) j -> p c j i", i=4),
+                src.rearrange("p j (c i) -> p c j i", i=4),
+            )
+
+        def quantize(codes, scales, woven):
+            nc.vector.quantize_mx(out=codes.bitcast(FP8X4), scales=scales, in_=woven)
+
+        got_scales = tile("got_scales", [P, I], U8)
+        got_words = tile("got_words", [P, I], U16)
+        emb_sc = tile("emb_sc", [P, PACK, P], U8)
+        emb_w = tile("emb_w", [P, PACK, P], U16)
+        nc.vector.tensor_copy(got_scales[:], store_scales[:].indirect(offsets[:]))
+        nc.vector.tensor_copy(
+            emb_sc[:].rearrange("p r s -> p s r"), got_scales[:].rearrange("p (s r) -> p s r", r=PACK)
+        )
+        nc.vector.tensor_copy(got_words[:], store_words[:].indirect(offsets[:]))
+        nc.vector.tensor_copy(
+            emb_w[:].rearrange("p r s -> p s r"), got_words[:].rearrange("p (s r) -> p s r", r=PACK)
+        )
+
+        wi_codes, wi_scales = [], []
+        for h, copy in enumerate((nc.scalar.copy, nc.vector.tensor_copy)):
+            woven = tile("wi_woven%d" % h, [P, HALF, PACK], BF16)
+            codes = tile("wi_codes%d" % h, [P, HALF], U32)
+            scales = tile("wi_scales%d" % h, [P, HALF], U8)
+            weave(copy, woven[:], wi_raw[h][:])
+            quantize(codes[:], scales[:], woven[:].rearrange("p c j -> p (c j)"))
+            wi_codes.append(codes)
+            wi_scales.append(scales)
+
+        hs = tile("hs", [P, PACK, P, PACK], BF16)
+        for c in range(4):
+            bank = ps.tile([P, PACK, P], F32, name="g1_%d" % c)
+            cols = slice((c % 2) * P, (c % 2 + 1) * P)
+            for r in range(PACK):
+                nc.tensor.matmul_mx(
+                    out=bank[:, r, :],
+                    lhsT=emb_w[:, r, :].bitcast(FP4X4),
+                    lhsT_scale=emb_sc[:, r, :],
+                    rhs=wi_codes[c // 2][:, cols].bitcast(FP8X4),
+                    rhs_scale=wi_scales[c // 2][:, cols],
+                    start=True,
+                    stop=True,
+                )
+            h1 = tile("h1_%d" % c, [P, PACK, 32, PACK], F32)
+            nc.scalar.activation(h1[:], bank[:].rearrange("p r (m t) -> p t m r", t=PACK), ACT.Tanh)
+            nc.vector.tensor_tensor(
+                hs[:, :, 32 * c : 32 * (c + 1), :],
+                h1[:],
+                isc_sb.unsqueeze(1).unsqueeze(1).to_broadcast([P, PACK, 32, PACK]),
+                ALU.mult,
+            )
+
+        q_woven = tile("q_woven", [P, Q, PACK], BF16)
+        q_codes = tile("q_codes", [P, Q], U32)
+        q_scales = tile("q_scales", [P, Q], U8)
+        weave(nc.scalar.copy, q_woven[:], qemb_raw)
+        quantize(q_codes[:], q_scales[:], q_woven[:].rearrange("p c j -> p (c j)"))
+        wq_woven = tile("wq_woven", [P, PACK, P, PACK], BF16)
+        wq_codes = tile("wq_codes", [P, B], U32)
+        wq_scales = tile("wq_scales", [P, B], U8)
+        for h, copy in enumerate((nc.vector.tensor_copy, nc.scalar.copy)):
+            copy(
+                wq_woven[:, :, 64 * h : 64 * (h + 1), :].rearrange("p t m j -> p m j t"),
+                wq_raw[h].rearrange("p j (m t) -> p m j t", t=PACK),
+            )
+        quantize(wq_codes[:], wq_scales[:], wq_woven[:].rearrange("p t m j -> p (t m j)"))
+        z = ps.tile([P, PACK, Q], F32, name="z")
+        for t in range(PACK):
+            nc.tensor.matmul_mx(
+                out=z[:, t, :],
+                lhsT=wq_codes[:, t * P : (t + 1) * P].bitcast(FP8X4),
+                lhsT_scale=wq_scales[:, t * P : (t + 1) * P],
+                rhs=q_codes[:].bitcast(FP8X4),
+                rhs_scale=q_scales[:],
+                start=True,
+                stop=True,
+            )
+        tz = tile("tz", [P, PACK, Q], F32)
+        sq = tile("sq", [P, PACK, Q], F32)
+        nc.scalar.activation(tz[:], z[:], ACT.Tanh)
+        nc.scalar.activation(sq[:], tz[:], ACT.Square)
+        neg_gain = tile("neg_gain", [P, PACK], F32)
+        nc.vector.tensor_scalar(neg_gain[:], gain_sb, -1.0, None, ALU.mult)
+
+        d_woven = tile("d_woven", [P, Q, PACK], BF16)
+        d_codes = tile("d_codes", [P, Q], U32)
+        d_scales = tile("d_scales", [P, Q], U8)
+        weave(nc.scalar.copy, d_woven[:], dsc_raw)
+        quantize(d_codes[:], d_scales[:], d_woven[:].rearrange("p c j -> p (c j)"))
+        hs_codes = tile("hs_codes", [P, B], U32)
+        hs_scales = tile("hs_scales", [P, B], U8)
+        quantize(hs_codes[:], hs_scales[:], hs[:].rearrange("p t m r -> p (t m r)"))
+        gh = ps.tile([P, PACK, Q], F32, name="gh")
+        for t in range(PACK):
+            nc.tensor.matmul_mx(
+                out=gh[:, t, :],
+                lhsT=hs_codes[:, t * P : (t + 1) * P].bitcast(FP8X4),
+                lhsT_scale=hs_scales[:, t * P : (t + 1) * P],
+                rhs=d_codes[:].bitcast(FP8X4),
+                rhs_scale=d_scales[:],
+                start=True,
+                stop=True,
+            )
+
+        part = tile("part", [P, PACK, Q], F32)
+        y = tile("y", [P, PACK, Q], F32)
+        nc.vector.scalar_tensor_tensor(part[:], sq[:], 1.0, gh[:], ALU.subtract, ALU.mult)
+        for t in range(PACK):
+            nc.vector.scalar_tensor_tensor(
+                y[:, t, :], part[:, t, :], neg_gain[:, t : t + 1], old_sb[:, t, :], ALU.mult, ALU.add
+            )
+        nc.sync.dma_start(rows4(out_0), y[:])
+        y_woven = tile("y_woven", [P, Q, PACK], BF16)
+        y_codes = tile("y_codes", [P, Q], U32)
+        y_scales = tile("y_scales", [P, Q], U8)
+        weave(nc.vector.tensor_copy, y_woven[:], y[:])
+        quantize(y_codes[:], y_scales[:], y_woven[:].rearrange("p c j -> p (c j)"))
+        nc.sync.dma_start(out_1[0].rearrange("p c r -> p (c r)").bitcast(I32), y_codes[:].bitcast(I32))
+        for g in range(4):
+            queue = nc.scalar if g % 2 == 0 else nc.sync
+            queue.dma_start(
+                out_2[0, 4 * g : 4 * g + 4, :].bitcast(I32),
+                y_scales[32 * g : 32 * g + 4, :].bitcast(I32),
+            )

@@ -35,44 +35,6 @@ def tile_attend_bsoftcodes_pl_kernel(
         def rows4(src):
             return src.rearrange("(p j) w -> p j w", j=PACK)
 
-        offsets = tile("offsets", [P, I // 16], U16)
-        store_scales = tile("store_scales", [P, T], U8)
-        store_words = tile("store_words", [P, T], U16)
-        wi_raw = [tile("wi_raw%d" % h, [P, PACK, HALF], F32) for h in range(2)]
-        warm_in = sb.tile([P, 1], F32, name="warm_in", tag="late", align_bytes=64)
-        warm_out = tile("warm_out", [P, 1], F32)
-
-        nc.vector.memset(store_scales[:].bitcast(I32), 0)
-        nc.vector.memset(warm_in[:], 0.0)
-        nc.sync.dma_start(offsets[:], offs)
-        for g in range(4):
-            nc.scalar.dma_start(
-                store_scales[32 * g : 32 * g + 4, :].bitcast(I32),
-                emb_scales[0, 4 * g : 4 * g + 4, :].bitcast(I32),
-            )
-        nc.sync.dma_start(store_words[:].bitcast(I32), emb_words[0].bitcast(I32))
-        for h in range(2):
-            nc.sync.dma_start(wi_raw[h][:], rows4(wi[:, h * HALF : (h + 1) * HALF]))
-        nc.scalar.activation(warm_out[:], warm_in[:], ACT.Tanh)
-
-        late = sb.tile([P, 2 * PACK * HALF + 3 * PACK * Q + 16], F32, name="late", tag="late", align_bytes=64)
-
-        def part_of_late(start, width):
-            return late[:, start : start + PACK * width].rearrange("p (j w) -> p j w", j=PACK)
-
-        wq_raw = [part_of_late(h * PACK * HALF, HALF) for h in range(2)]
-        qemb_raw, dsc_raw, old_sb = [part_of_late(PACK * B + n * PACK * Q, Q) for n in range(3)]
-        vectors = PACK * B + 3 * PACK * Q
-        isc_sb = late[:, vectors : vectors + PACK]
-        gain_sb = late[:, vectors + 8 : vectors + 8 + PACK]
-        nc.sync.dma_start(isc_sb, isc.rearrange("(p j) o -> p (j o)", j=PACK))
-        nc.sync.dma_start(qemb_raw, rows4(qemb))
-        for h in range(2):
-            nc.sync.dma_start(wq_raw[h], rows4(wq[:, h * HALF : (h + 1) * HALF]))
-        nc.sync.dma_start(dsc_raw, rows4(dsc))
-        nc.sync.dma_start(gain_sb, gain.rearrange("(p j) o -> p (j o)", j=PACK))
-        nc.sync.dma_start(old_sb, rows4(old))
-
         def weave(copy, dst, src):
             copy(
                 dst.rearrange("p (c i) j -> p c j i", i=4),
@@ -82,111 +44,169 @@ def tile_attend_bsoftcodes_pl_kernel(
         def quantize(codes, scales, woven):
             nc.vector.quantize_mx(out=codes.bitcast(FP8X4), scales=scales, in_=woven)
 
+        def product(out, lhs, lhs_scales, rhs, rhs_scales):
+            nc.tensor.matmul_mx(
+                out=out, lhsT=lhs, lhsT_scale=lhs_scales, rhs=rhs, rhs_scale=rhs_scales, start=True, stop=True
+            )
+
+        offsets = tile("offsets", [P, I // 16], U16)
+        store_scales = tile("store_scales", [P, T], U8)
+        store_words = tile("store_words", [P, T], U16)
+        warm_in = sb.tile([P, 1], F32, name="warm_in", tag="raw", align_bytes=64)
+        warm_out = tile("warm_out", [P, 1], F32)
+
+        nc.vector.memset(warm_in[:], 0.0)
+        nc.vector.memset(store_scales[:].bitcast(I32), 0)
+        nc.scalar.activation(warm_out[:], warm_in[:], ACT.Tanh)
+        nc.sync.dma_start(offsets[:], offs)
+        nc.sync.dma_start(store_words[:].bitcast(I32), emb_words[0].bitcast(I32))
+        qemb_raw = tile("qemb_raw", [P, PACK, Q], F32)
+        dsc_raw = tile("dsc_raw", [P, PACK, Q], F32)
+        nc.sync.dma_start(qemb_raw[:], rows4(qemb))
+        nc.sync.dma_start(dsc_raw[:], rows4(dsc))
+        for g in range(4):
+            nc.sync.dma_start(
+                store_scales[32 * g : 32 * g + 4, :].bitcast(I32),
+                emb_scales[0, 4 * g : 4 * g + 4, :].bitcast(I32),
+            )
+
+        raw = sb.tile([P, 2 * PACK * B + PACK * Q + 16], F32, name="raw", tag="raw", align_bytes=64)
+
+        def part_of_raw(start, width):
+            return raw[:, start : start + PACK * width].rearrange("p (j w) -> p j w", j=PACK)
+
+        wi_raw = [part_of_raw(h * PACK * HALF, HALF) for h in range(2)]
+        wq_raw = [part_of_raw(PACK * B + h * PACK * HALF, HALF) for h in range(2)]
+        old_sb = part_of_raw(2 * PACK * B, Q)
+        vectors = 2 * PACK * B + PACK * Q
+        isc_sb = raw[:, vectors : vectors + PACK]
+        gain_sb = raw[:, vectors + 8 : vectors + 8 + PACK]
+        for h in range(2):
+            nc.sync.dma_start(wi_raw[h], rows4(wi[:, h * HALF : (h + 1) * HALF]))
+        nc.sync.dma_start(isc_sb, isc.rearrange("(p j) o -> p (j o)", j=PACK))
+        for h in range(2):
+            nc.sync.dma_start(wq_raw[h], rows4(wq[:, h * HALF : (h + 1) * HALF]))
+        nc.sync.dma_start(gain_sb, gain.rearrange("(p j) o -> p (j o)", j=PACK))
+        nc.sync.dma_start(old_sb, rows4(old))
+
         got_scales = tile("got_scales", [P, I], U8)
         got_words = tile("got_words", [P, I], U16)
         emb_sc = tile("emb_sc", [P, PACK, P], U8)
         emb_w = tile("emb_w", [P, PACK, P], U16)
-        nc.vector.tensor_copy(got_scales[:], store_scales[:].indirect(offsets[:]))
-        nc.vector.tensor_copy(
-            emb_sc[:].rearrange("p r s -> p s r"), got_scales[:].rearrange("p (s r) -> p s r", r=PACK)
-        )
         nc.vector.tensor_copy(got_words[:], store_words[:].indirect(offsets[:]))
+        nc.vector.tensor_copy(got_scales[:], store_scales[:].indirect(offsets[:]))
         nc.vector.tensor_copy(
             emb_w[:].rearrange("p r s -> p s r"), got_words[:].rearrange("p (s r) -> p s r", r=PACK)
         )
+        nc.vector.tensor_copy(
+            emb_sc[:].rearrange("p r s -> p s r"), got_scales[:].rearrange("p (s r) -> p s r", r=PACK)
+        )
+
+        qd_woven = tile("qd_woven", [P, 2, Q, PACK], BF16)
+        qd_codes = tile("qd_codes", [P, 2, Q], U32)
+        qd_scales = tile("qd_scales", [P, 2, Q], U8)
+        weave(nc.scalar.copy, qd_woven[:, 0, :, :], qemb_raw[:])
+        weave(nc.scalar.copy, qd_woven[:, 1, :, :], dsc_raw[:])
 
         wi_codes, wi_scales = [], []
-        for h, copy in enumerate((nc.scalar.copy, nc.vector.tensor_copy)):
+        for h in range(2):
             woven = tile("wi_woven%d" % h, [P, HALF, PACK], BF16)
             codes = tile("wi_codes%d" % h, [P, HALF], U32)
             scales = tile("wi_scales%d" % h, [P, HALF], U8)
-            weave(copy, woven[:], wi_raw[h][:])
+            weave(nc.scalar.copy, woven[:], wi_raw[h])
             quantize(codes[:], scales[:], woven[:].rearrange("p c j -> p (c j)"))
             wi_codes.append(codes)
             wi_scales.append(scales)
 
+        quantize(
+            qd_codes[:].rearrange("p n c -> p (n c)"),
+            qd_scales[:].rearrange("p n c -> p (n c)"),
+            qd_woven[:].rearrange("p n c j -> p (n c j)"),
+        )
+        wq_woven = tile("wq_woven", [P, PACK, P, PACK], BF16)
+
+        def weave_wq(copy, h, m0, m1):
+            copy(
+                wq_woven[:, :, 64 * h + m0 : 64 * h + m1, :].rearrange("p t m j -> p m j t"),
+                wq_raw[h][:, :, PACK * m0 : PACK * m1].rearrange("p j (m t) -> p m j t", t=PACK),
+            )
+
+        weave_wq(nc.vector.tensor_copy, 0, 0, 64)
+
+        h1s = []
         hs = tile("hs", [P, PACK, P, PACK], BF16)
         for c in range(4):
             bank = ps.tile([P, PACK, P], F32, name="g1_%d" % c)
             cols = slice((c % 2) * P, (c % 2 + 1) * P)
             for r in range(PACK):
-                nc.tensor.matmul_mx(
-                    out=bank[:, r, :],
-                    lhsT=emb_w[:, r, :].bitcast(FP4X4),
-                    lhsT_scale=emb_sc[:, r, :],
-                    rhs=wi_codes[c // 2][:, cols].bitcast(FP8X4),
-                    rhs_scale=wi_scales[c // 2][:, cols],
-                    start=True,
-                    stop=True,
+                product(
+                    bank[:, r, :], emb_w[:, r, :].bitcast(FP4X4), emb_sc[:, r, :],
+                    wi_codes[c // 2][:, cols].bitcast(FP8X4), wi_scales[c // 2][:, cols],
                 )
             h1 = tile("h1_%d" % c, [P, PACK, 32, PACK], F32)
             nc.scalar.activation(h1[:], bank[:].rearrange("p r (m t) -> p t m r", t=PACK), ACT.Tanh)
+            h1s.append(h1)
+            if c == 1:
+                weave_wq(nc.scalar.copy, 1, 0, 64)
+        wq_codes, wq_scales = [], []
+        for u in range(2):
+            codes = tile("wq_codes%d" % u, [P, 2 * P], U32)
+            scales = tile("wq_scales%d" % u, [P, 2 * P], U8)
+            quantize(codes[:], scales[:], wq_woven[:, 2 * u : 2 * u + 2, :, :].rearrange("p t m j -> p (t m j)"))
+            wq_codes.append(codes)
+            wq_scales.append(scales)
+        for c in range(4):
             nc.vector.tensor_tensor(
                 hs[:, :, 32 * c : 32 * (c + 1), :],
-                h1[:],
+                h1s[c][:],
                 isc_sb.unsqueeze(1).unsqueeze(1).to_broadcast([P, PACK, 32, PACK]),
                 ALU.mult,
             )
 
-        q_woven = tile("q_woven", [P, Q, PACK], BF16)
-        q_codes = tile("q_codes", [P, Q], U32)
-        q_scales = tile("q_scales", [P, Q], U8)
-        weave(nc.scalar.copy, q_woven[:], qemb_raw)
-        quantize(q_codes[:], q_scales[:], q_woven[:].rearrange("p c j -> p (c j)"))
-        wq_woven = tile("wq_woven", [P, PACK, P, PACK], BF16)
-        wq_codes = tile("wq_codes", [P, B], U32)
-        wq_scales = tile("wq_scales", [P, B], U8)
-        for h, copy in enumerate((nc.vector.tensor_copy, nc.scalar.copy)):
-            copy(
-                wq_woven[:, :, 64 * h : 64 * (h + 1), :].rearrange("p t m j -> p m j t"),
-                wq_raw[h].rearrange("p j (m t) -> p m j t", t=PACK),
-            )
-        quantize(wq_codes[:], wq_scales[:], wq_woven[:].rearrange("p t m j -> p (t m j)"))
-        z = ps.tile([P, PACK, Q], F32, name="z")
-        for t in range(PACK):
-            nc.tensor.matmul_mx(
-                out=z[:, t, :],
-                lhsT=wq_codes[:, t * P : (t + 1) * P].bitcast(FP8X4),
-                lhsT_scale=wq_scales[:, t * P : (t + 1) * P],
-                rhs=q_codes[:].bitcast(FP8X4),
-                rhs_scale=q_scales[:],
-                start=True,
-                stop=True,
-            )
         tz = tile("tz", [P, PACK, Q], F32)
         sq = tile("sq", [P, PACK, Q], F32)
-        nc.scalar.activation(tz[:], z[:], ACT.Tanh)
-        nc.scalar.activation(sq[:], tz[:], ACT.Square)
+        slope = tile("slope", [P, PACK, Q], F32)
         neg_gain = tile("neg_gain", [P, PACK], F32)
-        nc.vector.tensor_scalar(neg_gain[:], gain_sb, -1.0, None, ALU.mult)
+        nc.scalar.activation(neg_gain[:], gain_sb, ACT.Copy, scale=-1.0)
+        for u in range(2):
+            z = ps.tile([P, 2, Q], F32, name="z%d" % u)
+            for t in range(2):
+                cols = slice(t * P, (t + 1) * P)
+                product(
+                    z[:, t, :], wq_codes[u][:, cols].bitcast(FP8X4), wq_scales[u][:, cols],
+                    qd_codes[:, 0, :].bitcast(FP8X4), qd_scales[:, 0, :],
+                )
+            nc.scalar.activation(tz[:, 2 * u : 2 * u + 2, :], z[:], ACT.Tanh)
+        for u in range(2):
+            pair = slice(2 * u, 2 * u + 2)
+            nc.scalar.activation(sq[:, pair, :], tz[:, pair, :], ACT.Square)
+            for t in range(2 * u, 2 * u + 2):
+                nc.scalar.activation(
+                    slope[:, t, :], sq[:, t, :], ACT.Identity,
+                    bias=gain_sb[:, t : t + 1], scale=neg_gain[:, t : t + 1],
+                )
 
-        d_woven = tile("d_woven", [P, Q, PACK], BF16)
-        d_codes = tile("d_codes", [P, Q], U32)
-        d_scales = tile("d_scales", [P, Q], U8)
-        weave(nc.scalar.copy, d_woven[:], dsc_raw)
-        quantize(d_codes[:], d_scales[:], d_woven[:].rearrange("p c j -> p (c j)"))
-        hs_codes = tile("hs_codes", [P, B], U32)
-        hs_scales = tile("hs_scales", [P, B], U8)
-        quantize(hs_codes[:], hs_scales[:], hs[:].rearrange("p t m r -> p (t m r)"))
-        gh = ps.tile([P, PACK, Q], F32, name="gh")
-        for t in range(PACK):
-            nc.tensor.matmul_mx(
-                out=gh[:, t, :],
-                lhsT=hs_codes[:, t * P : (t + 1) * P].bitcast(FP8X4),
-                lhsT_scale=hs_scales[:, t * P : (t + 1) * P],
-                rhs=d_codes[:].bitcast(FP8X4),
-                rhs_scale=d_scales[:],
-                start=True,
-                stop=True,
-            )
+        gh = []
+        for u in range(2):
+            codes = tile("hs_codes%d" % u, [P, 2 * P], U32)
+            scales = tile("hs_scales%d" % u, [P, 2 * P], U8)
+            quantize(codes[:], scales[:], hs[:, 2 * u : 2 * u + 2, :, :].rearrange("p t m r -> p (t m r)"))
+            bank = ps.tile([P, 2, Q], F32, name="gh%d" % u)
+            for t in range(2):
+                cols = slice(t * P, (t + 1) * P)
+                product(
+                    bank[:, t, :], codes[:, cols].bitcast(FP8X4), scales[:, cols],
+                    qd_codes[:, 1, :].bitcast(FP8X4), qd_scales[:, 1, :],
+                )
+            gh.append(bank)
 
         part = tile("part", [P, PACK, Q], F32)
         y = tile("y", [P, PACK, Q], F32)
-        nc.vector.scalar_tensor_tensor(part[:], sq[:], 1.0, gh[:], ALU.subtract, ALU.mult)
-        for t in range(PACK):
-            nc.vector.scalar_tensor_tensor(
-                y[:, t, :], part[:, t, :], neg_gain[:, t : t + 1], old_sb[:, t, :], ALU.mult, ALU.add
-            )
+        for u in range(2):
+            nc.vector.tensor_tensor(part[:, 2 * u : 2 * u + 2, :], gh[u][:], slope[:, 2 * u : 2 * u + 2, :], ALU.mult)
+        for u in range(2):
+            pair = slice(2 * u, 2 * u + 2)
+            nc.vector.tensor_tensor(y[:, pair, :], part[:, pair, :], old_sb[:, pair, :], ALU.add)
         nc.sync.dma_start(rows4(out_0), y[:])
         y_woven = tile("y_woven", [P, Q, PACK], BF16)
         y_codes = tile("y_codes", [P, Q], U32)

@@ -50,163 +50,142 @@ def tile_attend_bsoftcodes_pl_kernel(
             )
 
         offsets = tile("offsets", [P, I // 16], U16)
-        store_scales = tile("store_scales", [P, T], U8)
+        store_scales = sb.tile([P, T], U8, name="store_scales", tag="store_scales", align_bytes=64)
         store_words = tile("store_words", [P, T], U16)
         warm_in = sb.tile([P, 1], F32, name="warm_in", tag="raw", align_bytes=64)
         warm_out = tile("warm_out", [P, 1], F32)
+        wi_first = tile("wi_first", [P, PACK, HALF], F32)
 
         nc.vector.memset(warm_in[:], 0.0)
         nc.vector.memset(store_scales[:].bitcast(I32), 0)
         nc.scalar.activation(warm_out[:], warm_in[:], ACT.Tanh)
         nc.sync.dma_start(offsets[:], offs)
         nc.sync.dma_start(store_words[:].bitcast(I32), emb_words[0].bitcast(I32))
-        qemb_raw = tile("qemb_raw", [P, PACK, Q], F32)
-        dsc_raw = tile("dsc_raw", [P, PACK, Q], F32)
-        nc.sync.dma_start(qemb_raw[:], rows4(qemb))
-        nc.sync.dma_start(dsc_raw[:], rows4(dsc))
+        nc.sync.dma_start(wi_first[:], rows4(wi[:, 0:HALF]))
         for g in range(4):
             nc.sync.dma_start(
                 store_scales[32 * g : 32 * g + 4, :].bitcast(I32),
                 emb_scales[0, 4 * g : 4 * g + 4, :].bitcast(I32),
             )
 
-        raw = sb.tile([P, 2 * PACK * B + PACK * Q + 16], F32, name="raw", tag="raw", align_bytes=64)
+        raw = sb.tile([P, 3 * PACK * HALF + 3 * PACK * Q + 16], F32, name="raw", tag="raw", align_bytes=64)
 
         def part_of_raw(start, width):
             return raw[:, start : start + PACK * width].rearrange("p (j w) -> p j w", j=PACK)
 
-        wi_raw = [part_of_raw(h * PACK * HALF, HALF) for h in range(2)]
-        wq_raw = [part_of_raw(PACK * B + h * PACK * HALF, HALF) for h in range(2)]
-        old_sb = part_of_raw(2 * PACK * B, Q)
-        vectors = 2 * PACK * B + PACK * Q
+        wi_raw = [wi_first[:], part_of_raw(0, HALF)]
+        wq_raw = [part_of_raw((h + 1) * PACK * HALF, HALF) for h in range(2)]
+        qemb_raw, dsc_raw, old_sb = [part_of_raw(3 * PACK * HALF + n * PACK * Q, Q) for n in range(3)]
+        vectors = 3 * PACK * HALF + 3 * PACK * Q
         isc_sb = raw[:, vectors : vectors + PACK]
         gain_sb = raw[:, vectors + 8 : vectors + 8 + PACK]
-        for h in range(2):
-            nc.sync.dma_start(wi_raw[h], rows4(wi[:, h * HALF : (h + 1) * HALF]))
+        nc.sync.dma_start(wi_raw[1], rows4(wi[:, HALF:B]))
+        nc.sync.dma_start(qemb_raw, rows4(qemb))
+        nc.sync.dma_start(wq_raw[0], rows4(wq[:, 0:HALF]))
         nc.sync.dma_start(isc_sb, isc.rearrange("(p j) o -> p (j o)", j=PACK))
-        for h in range(2):
-            nc.sync.dma_start(wq_raw[h], rows4(wq[:, h * HALF : (h + 1) * HALF]))
+        nc.sync.dma_start(wq_raw[1], rows4(wq[:, HALF:B]))
+        nc.sync.dma_start(dsc_raw, rows4(dsc))
         nc.sync.dma_start(gain_sb, gain.rearrange("(p j) o -> p (j o)", j=PACK))
         nc.sync.dma_start(old_sb, rows4(old))
 
+        def weave_dealt(copy, dst, src):
+            copy(dst.rearrange("p t m j -> p m j t"), src.rearrange("p j (m t) -> p m j t", t=PACK))
+
+        def flat(ap):
+            return ap.rearrange("p t m j -> p (t m j)")
+
+        def mx_tiles(name, width):
+            return tile(name + "_codes", [P, width], U32), tile(name + "_scales", [P, width], U8)
+
+        def mx_cols(operand, n):
+            codes, scales = operand
+            return codes[:, n * P : (n + 1) * P].bitcast(FP8X4), scales[:, n * P : (n + 1) * P]
+
         got_scales = tile("got_scales", [P, I], U8)
-        got_words = tile("got_words", [P, I], U16)
-        emb_sc = tile("emb_sc", [P, PACK, P], U8)
-        emb_w = tile("emb_w", [P, PACK, P], U16)
+        got_words = sb.tile([P, I], U16, name="got_words", tag="got_words", align_bytes=64)
         nc.vector.tensor_copy(got_words[:], store_words[:].indirect(offsets[:]))
         nc.vector.tensor_copy(got_scales[:], store_scales[:].indirect(offsets[:]))
-        nc.vector.tensor_copy(
-            emb_w[:].rearrange("p r s -> p s r"), got_words[:].rearrange("p (s r) -> p s r", r=PACK)
-        )
-        nc.vector.tensor_copy(
-            emb_sc[:].rearrange("p r s -> p s r"), got_scales[:].rearrange("p (s r) -> p s r", r=PACK)
-        )
 
-        qd_woven = tile("qd_woven", [P, 2, Q, PACK], BF16)
-        qd_codes = tile("qd_codes", [P, 2, Q], U32)
-        qd_scales = tile("qd_scales", [P, 2, Q], U8)
-        weave(nc.scalar.copy, qd_woven[:, 0, :, :], qemb_raw[:])
-        weave(nc.scalar.copy, qd_woven[:, 1, :, :], dsc_raw[:])
-
-        wi_codes, wi_scales = [], []
+        wi_woven = [tile("wi_woven%d" % h, [P, PACK, 64, PACK], BF16) for h in range(2)]
+        emb_sc = tile("emb_sc", [P, PACK, P], U8)
+        emb_w = sb.tile([P, PACK, P], U16, name="emb_w", tag="store_scales", align_bytes=64)
+        nc.vector.tensor_copy(emb_w[:], got_words[:].rearrange("p (s r) -> p r s", r=PACK))
+        nc.vector.tensor_copy(emb_sc[:], got_scales[:].rearrange("p (s r) -> p r s", r=PACK))
+        wi0_codes = sb.tile([P, HALF], U32, name="wi0_codes", tag="got_words", align_bytes=64)
+        wi_mx = [(wi0_codes, tile("wi0_scales", [P, HALF], U8)), mx_tiles("wi1", HALF)]
         for h in range(2):
-            woven = tile("wi_woven%d" % h, [P, HALF, PACK], BF16)
-            codes = tile("wi_codes%d" % h, [P, HALF], U32)
-            scales = tile("wi_scales%d" % h, [P, HALF], U8)
-            weave(nc.scalar.copy, woven[:], wi_raw[h])
-            quantize(codes[:], scales[:], woven[:].rearrange("p c j -> p (c j)"))
-            wi_codes.append(codes)
-            wi_scales.append(scales)
+            weave_dealt(nc.scalar.copy, wi_woven[h][:], wi_raw[h])
+        quantize(wi_mx[0][0][:], wi_mx[0][1][:], flat(wi_woven[0][:]))
+        quantize(wi_mx[1][0][:], wi_mx[1][1][:], flat(wi_woven[1][:]))
 
-        quantize(
-            qd_codes[:].rearrange("p n c -> p (n c)"),
-            qd_scales[:].rearrange("p n c -> p (n c)"),
-            qd_woven[:].rearrange("p n c j -> p (n c j)"),
-        )
+        q_woven = tile("q_woven", [P, Q, PACK], BF16)
+        q_mx = mx_tiles("q", Q)
+        weave(nc.scalar.copy, q_woven[:], qemb_raw)
         wq_woven = tile("wq_woven", [P, PACK, P, PACK], BF16)
 
         def weave_wq(copy, h, m0, m1):
-            copy(
-                wq_woven[:, :, 64 * h + m0 : 64 * h + m1, :].rearrange("p t m j -> p m j t"),
-                wq_raw[h][:, :, PACK * m0 : PACK * m1].rearrange("p j (m t) -> p m j t", t=PACK),
-            )
+            weave_dealt(copy, wq_woven[:, :, 64 * h + m0 : 64 * h + m1, :], wq_raw[h][:, :, PACK * m0 : PACK * m1])
 
         weave_wq(nc.vector.tensor_copy, 0, 0, 64)
+        weave_wq(nc.vector.tensor_copy, 1, 0, 32)
+        quantize(q_mx[0][:], q_mx[1][:], q_woven[:].rearrange("p c j -> p (c j)"))
 
-        h1s = []
-        hs = tile("hs", [P, PACK, P, PACK], BF16)
-        for c in range(4):
-            bank = ps.tile([P, PACK, P], F32, name="g1_%d" % c)
-            cols = slice((c % 2) * P, (c % 2 + 1) * P)
-            for r in range(PACK):
-                product(
-                    bank[:, r, :], emb_w[:, r, :].bitcast(FP4X4), emb_sc[:, r, :],
-                    wi_codes[c // 2][:, cols].bitcast(FP8X4), wi_scales[c // 2][:, cols],
-                )
-            h1 = tile("h1_%d" % c, [P, PACK, 32, PACK], F32)
-            nc.scalar.activation(h1[:], bank[:].rearrange("p r (m t) -> p t m r", t=PACK), ACT.Tanh)
-            h1s.append(h1)
-            if c == 1:
-                weave_wq(nc.scalar.copy, 1, 0, 64)
-        wq_codes, wq_scales = [], []
+        h1 = {}
+        d_woven = tile("d_woven", [P, Q, PACK], BF16)
+        d_mx = mx_tiles("d", Q)
         for u in range(2):
-            codes = tile("wq_codes%d" % u, [P, 2 * P], U32)
-            scales = tile("wq_scales%d" % u, [P, 2 * P], U8)
-            quantize(codes[:], scales[:], wq_woven[:, 2 * u : 2 * u + 2, :, :].rearrange("p t m j -> p (t m j)"))
-            wq_codes.append(codes)
-            wq_scales.append(scales)
-        for c in range(4):
-            nc.vector.tensor_tensor(
-                hs[:, :, 32 * c : 32 * (c + 1), :],
-                h1s[c][:],
-                isc_sb.unsqueeze(1).unsqueeze(1).to_broadcast([P, PACK, 32, PACK]),
-                ALU.mult,
-            )
+            for h in range(2):
+                bank = ps.tile([P, PACK, P], F32, name="g1_%d%d" % (h, u))
+                for r in range(PACK):
+                    product(bank[:, r, :], emb_w[:, r, :].bitcast(FP4X4), emb_sc[:, r, :], *mx_cols(wi_mx[h], u))
+                h1[h, u] = tile("h1_%d%d" % (h, u), [P, P, PACK], F32)
+                nc.scalar.activation(h1[h, u][:], bank[:].rearrange("p r n -> p n r"), ACT.Tanh)
+            if u == 0:
+                weave_wq(nc.scalar.copy, 1, 32, 64)
+                weave(nc.scalar.copy, d_woven[:], dsc_raw)
 
         tz = tile("tz", [P, PACK, Q], F32)
         sq = tile("sq", [P, PACK, Q], F32)
-        slope = tile("slope", [P, PACK, Q], F32)
         neg_gain = tile("neg_gain", [P, PACK], F32)
-        nc.scalar.activation(neg_gain[:], gain_sb, ACT.Copy, scale=-1.0)
         for u in range(2):
+            wq_mx = mx_tiles("wq%d" % u, 2 * P)
+            quantize(wq_mx[0][:], wq_mx[1][:], flat(wq_woven[:, 2 * u : 2 * u + 2, :, :]))
             z = ps.tile([P, 2, Q], F32, name="z%d" % u)
             for t in range(2):
-                cols = slice(t * P, (t + 1) * P)
-                product(
-                    z[:, t, :], wq_codes[u][:, cols].bitcast(FP8X4), wq_scales[u][:, cols],
-                    qd_codes[:, 0, :].bitcast(FP8X4), qd_scales[:, 0, :],
-                )
+                product(z[:, t, :], *mx_cols(wq_mx, t), *mx_cols(q_mx, 0))
             nc.scalar.activation(tz[:, 2 * u : 2 * u + 2, :], z[:], ACT.Tanh)
         for u in range(2):
             pair = slice(2 * u, 2 * u + 2)
             nc.scalar.activation(sq[:, pair, :], tz[:, pair, :], ACT.Square)
-            for t in range(2 * u, 2 * u + 2):
-                nc.scalar.activation(
-                    slope[:, t, :], sq[:, t, :], ACT.Identity,
-                    bias=gain_sb[:, t : t + 1], scale=neg_gain[:, t : t + 1],
-                )
+        nc.scalar.activation(neg_gain[:], gain_sb, ACT.Copy, scale=-1.0)
+        quantize(d_mx[0][:], d_mx[1][:], d_woven[:].rearrange("p c j -> p (c j)"))
 
         gh = []
         for u in range(2):
-            codes = tile("hs_codes%d" % u, [P, 2 * P], U32)
-            scales = tile("hs_scales%d" % u, [P, 2 * P], U8)
-            quantize(codes[:], scales[:], hs[:, 2 * u : 2 * u + 2, :, :].rearrange("p t m r -> p (t m r)"))
+            hs = tile("hs%d" % u, [P, 2, P, PACK], BF16)
+            for h in range(2):
+                nc.vector.tensor_tensor(
+                    hs[:, :, 64 * h : 64 * (h + 1), :],
+                    h1[h, u][:].rearrange("p (t m) r -> p t m r", t=2),
+                    isc_sb.unsqueeze(1).unsqueeze(1).to_broadcast([P, 2, 64, PACK]),
+                    ALU.mult,
+                )
+            hs_mx = mx_tiles("hs%d" % u, 2 * P)
+            quantize(hs_mx[0][:], hs_mx[1][:], flat(hs[:]))
             bank = ps.tile([P, 2, Q], F32, name="gh%d" % u)
             for t in range(2):
-                cols = slice(t * P, (t + 1) * P)
-                product(
-                    bank[:, t, :], codes[:, cols].bitcast(FP8X4), scales[:, cols],
-                    qd_codes[:, 1, :].bitcast(FP8X4), qd_scales[:, 1, :],
-                )
+                product(bank[:, t, :], *mx_cols(hs_mx, t), *mx_cols(d_mx, 0))
             gh.append(bank)
 
         part = tile("part", [P, PACK, Q], F32)
         y = tile("y", [P, PACK, Q], F32)
         for u in range(2):
-            nc.vector.tensor_tensor(part[:, 2 * u : 2 * u + 2, :], gh[u][:], slope[:, 2 * u : 2 * u + 2, :], ALU.mult)
-        for u in range(2):
             pair = slice(2 * u, 2 * u + 2)
-            nc.vector.tensor_tensor(y[:, pair, :], part[:, pair, :], old_sb[:, pair, :], ALU.add)
+            nc.vector.scalar_tensor_tensor(part[:, pair, :], sq[:, pair, :], 1.0, gh[u][:], ALU.subtract, ALU.mult)
+        for t in range(PACK):
+            nc.vector.scalar_tensor_tensor(
+                y[:, t, :], part[:, t, :], neg_gain[:, t : t + 1], old_sb[:, t, :], ALU.mult, ALU.add
+            )
         nc.sync.dma_start(rows4(out_0), y[:])
         y_woven = tile("y_woven", [P, Q, PACK], BF16)
         y_codes = tile("y_codes", [P, Q], U32)

@@ -135,7 +135,7 @@ def tile_attend_bsoftcodes_pl_kernel(
         d_mx = mx_tiles("d", Q)
         for u in range(2):
             for h in range(2):
-                bank = ps.tile([P, PACK, P], F32, name="g1_%d%d" % (h, u))
+                bank = ps.tile([P, PACK, P], F32, name="g1_%d%d" % (h, u), tag="g1_%d%d" % (h, u))
                 for r in range(PACK):
                     product(bank[:, r, :], emb_w[:, r, :].bitcast(FP4X4), emb_sc[:, r, :], *mx_cols(wi_mx[h], u))
                 h1[h, u] = tile("h1_%d%d" % (h, u), [P, P, PACK], F32)
@@ -160,38 +160,57 @@ def tile_attend_bsoftcodes_pl_kernel(
         nc.scalar.activation(neg_gain[:], gain_sb, ACT.Copy, scale=-1.0)
         quantize(d_mx[0][:], d_mx[1][:], d_woven[:].rearrange("p c j -> p (c j)"))
 
-        gh = []
-        for u in range(2):
-            hs = tile("hs%d" % u, [P, 2, P, PACK], BF16)
-            for h in range(2):
-                nc.vector.tensor_tensor(
-                    hs[:, :, 64 * h : 64 * (h + 1), :],
-                    h1[h, u][:].rearrange("p (t m) r -> p t m r", t=2),
-                    isc_sb.unsqueeze(1).unsqueeze(1).to_broadcast([P, 2, 64, PACK]),
-                    ALU.mult,
-                )
-            hs_mx = mx_tiles("hs%d" % u, 2 * P)
-            quantize(hs_mx[0][:], hs_mx[1][:], flat(hs[:]))
-            bank = ps.tile([P, 2, Q], F32, name="gh%d" % u)
-            for t in range(2):
-                product(bank[:, t, :], *mx_cols(hs_mx, t), *mx_cols(d_mx, 0))
-            gh.append(bank)
-
+        hs = tile("hs", [P, PACK, P, PACK], BF16)
         part = tile("part", [P, PACK, Q], F32)
         y = tile("y", [P, PACK, Q], F32)
-        for u in range(2):
-            pair = slice(2 * u, 2 * u + 2)
-            nc.vector.scalar_tensor_tensor(part[:, pair, :], sq[:, pair, :], 1.0, gh[u][:], ALU.subtract, ALU.mult)
-        for t in range(PACK):
+
+        def scale_slots(h, t0, t1):
+            u = t0 // 2
+            nc.vector.tensor_tensor(
+                hs[:, t0:t1, 64 * h : 64 * (h + 1), :],
+                h1[h, u][:].rearrange("p (t m) r -> p t m r", t=2)[:, t0 - 2 * u : t1 - 2 * u],
+                isc_sb.unsqueeze(1).unsqueeze(1).to_broadcast([P, t1 - t0, 64, PACK]),
+                ALU.mult,
+            )
+
+        def sum_slots(t0, t1, bank_tag):
+            hs_mx = mx_tiles("hs%d" % t0, (t1 - t0) * P)
+            quantize(hs_mx[0][:], hs_mx[1][:], flat(hs[:, t0:t1]))
+            bank = ps.tile([P, t1 - t0, Q], F32, name="gh%d" % t0, tag=bank_tag)
+            for t in range(t1 - t0):
+                product(bank[:, t, :], *mx_cols(hs_mx, t), *mx_cols(d_mx, 0))
+            return bank
+
+        def times_slope(t0, t1, bank):
+            nc.vector.scalar_tensor_tensor(part[:, t0:t1, :], sq[:, t0:t1, :], 1.0, bank[:], ALU.subtract, ALU.mult)
+
+        def finish(t):
             nc.vector.scalar_tensor_tensor(
                 y[:, t, :], part[:, t, :], neg_gain[:, t : t + 1], old_sb[:, t, :], ALU.mult, ALU.add
             )
+
+        scale_slots(0, 0, 2)
+        scale_slots(1, 0, 2)
+        gh01 = sum_slots(0, 2, "gh01")
+        scale_slots(0, 2, 4)
+        scale_slots(1, 2, 3)
+        scale_slots(1, 3, 4)
+        gh2 = sum_slots(2, 3, "gh2")
+        gh3 = sum_slots(3, 4, "g1_00")
+        times_slope(0, 2, gh01)
+        times_slope(2, 3, gh2)
+        times_slope(3, 4, gh3)
+        for t in range(PACK):
+            finish(t)
         nc.sync.dma_start(rows4(out_0), y[:])
-        y_woven = tile("y_woven", [P, Q, PACK], BF16)
+        y_woven = [tile("y_woven%d" % n, [P, Q // 2, PACK], BF16) for n in range(2)]
         y_codes = tile("y_codes", [P, Q], U32)
         y_scales = tile("y_scales", [P, Q], U8)
-        weave(nc.vector.tensor_copy, y_woven[:], y[:])
-        quantize(y_codes[:], y_scales[:], y_woven[:].rearrange("p c j -> p (c j)"))
+        for n, copy in enumerate((nc.scalar.copy, nc.vector.tensor_copy)):
+            weave(copy, y_woven[n][:], y[:, :, n * Q // 2 : (n + 1) * Q // 2])
+        for n in range(2):
+            cols = slice(n * Q // 2, (n + 1) * Q // 2)
+            quantize(y_codes[:, cols], y_scales[:, cols], y_woven[n][:].rearrange("p c j -> p (c j)"))
         nc.sync.dma_start(out_1[0].rearrange("p c r -> p (c r)").bitcast(I32), y_codes[:].bitcast(I32))
         for g in range(4):
             queue = nc.scalar if g % 2 == 0 else nc.sync

from contextlib import ExitStack

import concourse.mybir as mybir

K, B, T, I, Q = 512, 512, 2048, 512, 128
FLOPS = 2 * K * B * Q + 2 * K * B * I + 2 * I * B * Q

F32 = mybir.dt.float32
BF16 = mybir.dt.bfloat16
I32 = mybir.dt.int32
U32 = mybir.dt.uint32
U16 = mybir.dt.uint16
U8 = mybir.dt.uint8
FP8X4 = mybir.dt.float8_e4m3fn_x4
FP4X4 = mybir.dt.float4_e2m1fn_x4
ACT = mybir.ActivationFunctionType
ALU = mybir.AluOpType

P = 128
PACK = 4
HALF = B // 2


def tile_attend_bsoftcodes_pl_kernel(
    tc, qemb, wq, emb_words, emb_scales, wi, isc, dsc, gain, old, offs, out_0, out_1, out_2
):
    nc = tc.nc
    with ExitStack() as ctx:
        sb = ctx.enter_context(tc.tile_pool(name="sb", bufs=1))
        ps = ctx.enter_context(tc.psum_pool(name="ps", bufs=1))

        def tile(name, shape, dtype):
            return sb.tile(shape, dtype, name=name, align_bytes=64)

        def rows4(src):
            return src.rearrange("(p j) w -> p j w", j=PACK)

        def weave(copy, dst, src):
            copy(
                dst.rearrange("p (c i) j -> p c j i", i=4),
                src.rearrange("p j (c i) -> p c j i", i=4),
            )

        def quantize(codes, scales, woven):
            nc.vector.quantize_mx(out=codes.bitcast(FP8X4), scales=scales, in_=woven)

        def product(out, lhs, lhs_scales, rhs, rhs_scales):
            nc.tensor.matmul_mx(
                out=out, lhsT=lhs, lhsT_scale=lhs_scales, rhs=rhs, rhs_scale=rhs_scales, start=True, stop=True
            )

        offsets = tile("offsets", [P, I // 16], U16)
        store_scales = sb.tile([P, T], U8, name="store_scales", tag="store_scales", align_bytes=64)
        store_words = tile("store_words", [P, T], U16)
        warm_in = sb.tile([P, 1], F32, name="warm_in", tag="raw", align_bytes=64)
        warm_out = tile("warm_out", [P, 1], F32)
        wi_first = tile("wi_first", [P, PACK, HALF], F32)

        nc.vector.memset(warm_in[:], 0.0)
        nc.vector.memset(store_scales[:].bitcast(I32), 0)
        nc.scalar.activation(warm_out[:], warm_in[:], ACT.Tanh)
        nc.sync.dma_start(offsets[:], offs)
        nc.sync.dma_start(store_words[:].bitcast(I32), emb_words[0].bitcast(I32))
        nc.sync.dma_start(wi_first[:], rows4(wi[:, 0:HALF]))
        for g in range(4):
            nc.sync.dma_start(
                store_scales[32 * g : 32 * g + 4, :].bitcast(I32),
                emb_scales[0, 4 * g : 4 * g + 4, :].bitcast(I32),
            )

        raw = sb.tile([P, 3 * PACK * HALF + 3 * PACK * Q + 16], F32, name="raw", tag="raw", align_bytes=64)

        def part_of_raw(start, width):
            return raw[:, start : start + PACK * width].rearrange("p (j w) -> p j w", j=PACK)

        wi_raw = [wi_first[:], part_of_raw(0, HALF)]
        wq_raw = [part_of_raw((h + 1) * PACK * HALF, HALF) for h in range(2)]
        qemb_raw, dsc_raw, old_sb = [part_of_raw(3 * PACK * HALF + n * PACK * Q, Q) for n in range(3)]
        vectors = 3 * PACK * HALF + 3 * PACK * Q
        isc_sb = raw[:, vectors : vectors + PACK]
        gain_sb = raw[:, vectors + 8 : vectors + 8 + PACK]
        nc.sync.dma_start(wi_raw[1], rows4(wi[:, HALF:B]))
        nc.sync.dma_start(qemb_raw, rows4(qemb))
        nc.sync.dma_start(wq_raw[0], rows4(wq[:, 0:HALF]))
        nc.sync.dma_start(isc_sb, isc.rearrange("(p j) o -> p (j o)", j=PACK))
        nc.sync.dma_start(wq_raw[1], rows4(wq[:, HALF:B]))
        nc.sync.dma_start(dsc_raw, rows4(dsc))
        nc.sync.dma_start(gain_sb, gain.rearrange("(p j) o -> p (j o)", j=PACK))
        nc.sync.dma_start(old_sb, rows4(old))

        def weave_dealt(copy, dst, src):
            copy(dst.rearrange("p t m j -> p m j t"), src.rearrange("p j (m t) -> p m j t", t=PACK))

        def flat(ap):
            return ap.rearrange("p t m j -> p (t m j)")

        def mx_tiles(name, width):
            return tile(name + "_codes", [P, width], U32), tile(name + "_scales", [P, width], U8)

        def mx_cols(operand, n):
            codes, scales = operand
            return codes[:, n * P : (n + 1) * P].bitcast(FP8X4), scales[:, n * P : (n + 1) * P]

        got_scales = tile("got_scales", [P, I], U8)
        got_words = sb.tile([P, I], U16, name="got_words", tag="got_words", align_bytes=64)
        nc.vector.tensor_copy(got_words[:], store_words[:].indirect(offsets[:]))
        nc.vector.tensor_copy(got_scales[:], store_scales[:].indirect(offsets[:]))

        wi_woven = [tile("wi_woven%d" % h, [P, PACK, 64, PACK], BF16) for h in range(2)]
        emb_sc = tile("emb_sc", [P, PACK, P], U8)
        emb_w = sb.tile([P, PACK, P], U16, name="emb_w", tag="store_scales", align_bytes=64)
        nc.vector.tensor_copy(emb_w[:], got_words[:].rearrange("p (s r) -> p r s", r=PACK))
        nc.vector.tensor_copy(emb_sc[:], got_scales[:].rearrange("p (s r) -> p r s", r=PACK))
        wi0_codes = sb.tile([P, HALF], U32, name="wi0_codes", tag="got_words", align_bytes=64)
        wi_mx = [(wi0_codes, tile("wi0_scales", [P, HALF], U8)), mx_tiles("wi1", HALF)]
        for h in range(2):
            weave_dealt(nc.scalar.copy, wi_woven[h][:], wi_raw[h])
        quantize(wi_mx[0][0][:], wi_mx[0][1][:], flat(wi_woven[0][:]))
        quantize(wi_mx[1][0][:], wi_mx[1][1][:], flat(wi_woven[1][:]))

        q_woven = tile("q_woven", [P, Q, PACK], BF16)
        q_mx = mx_tiles("q", Q)
        weave(nc.scalar.copy, q_woven[:], qemb_raw)
        wq_woven = tile("wq_woven", [P, PACK, P, PACK], BF16)

        def weave_wq(copy, h, m0, m1):
            weave_dealt(copy, wq_woven[:, :, 64 * h + m0 : 64 * h + m1, :], wq_raw[h][:, :, PACK * m0 : PACK * m1])

        weave_wq(nc.vector.tensor_copy, 0, 0, 64)
        weave_wq(nc.vector.tensor_copy, 1, 0, 32)
        quantize(q_mx[0][:], q_mx[1][:], q_woven[:].rearrange("p c j -> p (c j)"))

        h1 = {}
        d_woven = tile("d_woven", [P, Q, PACK], BF16)
        d_mx = mx_tiles("d", Q)
        for u in range(2):
            for h in range(2):
                bank = ps.tile([P, PACK, P], F32, name="g1_%d%d" % (h, u), tag="g1_%d%d" % (h, u))
                for r in range(PACK):
                    product(bank[:, r, :], emb_w[:, r, :].bitcast(FP4X4), emb_sc[:, r, :], *mx_cols(wi_mx[h], u))
                h1[h, u] = tile("h1_%d%d" % (h, u), [P, P, PACK], F32)
                nc.scalar.activation(h1[h, u][:], bank[:].rearrange("p r n -> p n r"), ACT.Tanh)
            if u == 0:
                weave_wq(nc.scalar.copy, 1, 32, 64)
                weave(nc.scalar.copy, d_woven[:], dsc_raw)

        tz = tile("tz", [P, PACK, Q], F32)
        sq = tile("sq", [P, PACK, Q], F32)
        neg_gain = tile("neg_gain", [P, PACK], F32)
        for u in range(2):
            wq_mx = mx_tiles("wq%d" % u, 2 * P)
            quantize(wq_mx[0][:], wq_mx[1][:], flat(wq_woven[:, 2 * u : 2 * u + 2, :, :]))
            z = ps.tile([P, 2, Q], F32, name="z%d" % u)
            for t in range(2):
                product(z[:, t, :], *mx_cols(wq_mx, t), *mx_cols(q_mx, 0))
            nc.scalar.activation(tz[:, 2 * u : 2 * u + 2, :], z[:], ACT.Tanh)
        for u in range(2):
            pair = slice(2 * u, 2 * u + 2)
            nc.scalar.activation(sq[:, pair, :], tz[:, pair, :], ACT.Square)
        nc.scalar.activation(neg_gain[:], gain_sb, ACT.Copy, scale=-1.0)
        quantize(d_mx[0][:], d_mx[1][:], d_woven[:].rearrange("p c j -> p (c j)"))

        hs = tile("hs", [P, PACK, P, PACK], BF16)
        part = tile("part", [P, PACK, Q], F32)
        y = tile("y", [P, PACK, Q], F32)

        def scale_slots(h, t0, t1):
            u = t0 // 2
            nc.vector.tensor_tensor(
                hs[:, t0:t1, 64 * h : 64 * (h + 1), :],
                h1[h, u][:].rearrange("p (t m) r -> p t m r", t=2)[:, t0 - 2 * u : t1 - 2 * u],
                isc_sb.unsqueeze(1).unsqueeze(1).to_broadcast([P, t1 - t0, 64, PACK]),
                ALU.mult,
            )

        def sum_slots(t0, t1, bank_tag):
            hs_mx = mx_tiles("hs%d" % t0, (t1 - t0) * P)
            quantize(hs_mx[0][:], hs_mx[1][:], flat(hs[:, t0:t1]))
            bank = ps.tile([P, t1 - t0, Q], F32, name="gh%d" % t0, tag=bank_tag)
            for t in range(t1 - t0):
                product(bank[:, t, :], *mx_cols(hs_mx, t), *mx_cols(d_mx, 0))
            return bank

        def times_slope(t0, t1, bank):
            nc.vector.scalar_tensor_tensor(part[:, t0:t1, :], sq[:, t0:t1, :], 1.0, bank[:], ALU.subtract, ALU.mult)

        def finish(t):
            nc.vector.scalar_tensor_tensor(
                y[:, t, :], part[:, t, :], neg_gain[:, t : t + 1], old_sb[:, t, :], ALU.mult, ALU.add
            )

        scale_slots(0, 0, 2)
        scale_slots(1, 0, 2)
        gh01 = sum_slots(0, 2, "gh01")
        scale_slots(0, 2, 4)
        scale_slots(1, 2, 3)
        scale_slots(1, 3, 4)
        gh2 = sum_slots(2, 3, "gh2")
        gh3 = sum_slots(3, 4, "g1_00")
        times_slope(0, 2, gh01)
        times_slope(2, 3, gh2)
        times_slope(3, 4, gh3)
        for t in range(PACK):
            finish(t)
        nc.sync.dma_start(rows4(out_0), y[:])
        y_woven = [tile("y_woven%d" % n, [P, Q // 2, PACK], BF16) for n in range(2)]
        y_codes = tile("y_codes", [P, Q], U32)
        y_scales = tile("y_scales", [P, Q], U8)
        for n, copy in enumerate((nc.scalar.copy, nc.vector.tensor_copy)):
            weave(copy, y_woven[n][:], y[:, :, n * Q // 2 : (n + 1) * Q // 2])
        for n in range(2):
            cols = slice(n * Q // 2, (n + 1) * Q // 2)
            quantize(y_codes[:, cols], y_scales[:, cols], y_woven[n][:].rearrange("p c j -> p (c j)"))
        nc.sync.dma_start(out_1[0].rearrange("p c r -> p (c r)").bitcast(I32), y_codes[:].bitcast(I32))
        for g in range(4):
            queue = nc.scalar if g % 2 == 0 else nc.sync
            queue.dma_start(
                out_2[0, 4 * g : 4 * g + 4, :].bitcast(I32),
                y_scales[32 * g : 32 * g + 4, :].bitcast(I32),
            )
